import numpy as np
import ml_dtypes


def mxq(x, axis, fmt="e4m3"):
    dtype, down = {"e4m3": (ml_dtypes.float8_e4m3fn, 7), "e5m2": (ml_dtypes.float8_e5m2, 14)}[fmt]
    v = np.moveaxis(np.asarray(x, np.float32).astype(ml_dtypes.bfloat16).astype(np.float64), axis, -1)
    blocks = v.reshape(v.shape[:-1] + (-1, 32))
    amax = np.abs(blocks).max(-1, keepdims=True)
    byte = np.maximum(np.where(amax > 0, np.frexp(amax)[1] - 1 + 127, 0) - down, 1)
    scale = np.exp2(byte - 127.0)
    codes = (blocks / scale).astype(np.float32).astype(dtype).astype(np.float64)
    return np.moveaxis((codes * scale).reshape(v.shape), -1, axis)


WIDE = False


def mx_kscale(k):
    if not WIDE:
        return np.ones(k)
    levels = np.array([30, -30])
    if k % 512:
        return np.exp2(np.random.permutation(np.resize(levels, k // 32))).repeat(32)
    a = np.empty((k // 512, 16))
    for p in range(k // 512):
        a[p, :8] = np.random.permutation(np.resize(levels, 8))
        for g in range(8):
            far = levels[np.abs(levels - a[p, g]) >= 10]
            a[p, g + 8] = far[np.random.randint(len(far))]
    return np.exp2(a.ravel()).repeat(32)


def f64(x):
    return np.asarray(x).astype(np.float64)


def striped(idx):
    return np.tile(np.asarray(idx).reshape(-1, 16).T, (8, 1)).astype(np.uint16)


def unstriped(offs):
    return offs[:16].T.reshape(-1).astype(np.int64)


def striped8(idx):
    return np.asarray(idx).reshape(8, -1, 16).transpose(0, 2, 1).reshape(128, -1).astype(np.uint16)


def unstriped8(offs):
    return offs.reshape(8, 16, -1).transpose(0, 2, 1).reshape(8, -1).astype(np.int64)


def pick8(x, idx, run):
    r = np.arange(len(x))
    return x[r[:, None], idx[r % (8 * run) // run]]


E2M1 = np.array([0.0, 0.5, 1.0, 1.5, 2.0, 3.0, 4.0, 6.0, -0.0, -0.5, -1.0, -1.5, -2.0, -3.0, -4.0, -6.0])


def pack_weight(w, fmt):
    k, n = w.shape
    w = f64(np.asarray(w, np.float32).astype(ml_dtypes.bfloat16)).reshape(k // 32, 32, n)
    amax = np.abs(w).max(1)
    if fmt in ("e4m3", "e5m2"):
        byte = np.frexp(amax)[1] - 1 + 127 - (7 if fmt == "e4m3" else 14)
    else:
        mant, ex = np.frexp(amax / 6.0)
        byte = np.where(mant > 0.5, ex, ex - 1) + 127
    byte = np.clip(np.where(amax > 0, byte, 1), 1, 254)
    scaled = (w * np.exp2(127.0 - byte)[:, None, :]).reshape(k, n).astype(np.float32)
    by_word = np.ascontiguousarray(scaled.reshape(k // 512, 128, 4, n).transpose(0, 1, 3, 2))
    if fmt in ("e4m3", "e5m2"):
        words = by_word.astype(ml_dtypes.float8_e4m3fn if fmt == "e4m3" else ml_dtypes.float8_e5m2).view(np.uint8)
    else:
        c = by_word.astype(ml_dtypes.float4_e2m1fn).view(np.uint8) & 0xF
        words = (c[..., 0::2] | (c[..., 1::2] << 4)).reshape(k // 512, 128, 2 * n)
    return np.ascontiguousarray(words), np.ascontiguousarray(byte.astype(np.uint8).reshape(k // 512, 16, n))


def unpack_weight(words, scales, fmt):
    g, _, n = scales.shape
    words = np.ascontiguousarray(words).reshape(g, 128, n, -1)
    if fmt in ("e4m3", "e5m2"):
        vals = words.view(ml_dtypes.float8_e4m3fn if fmt == "e4m3" else ml_dtypes.float8_e5m2).astype(np.float64)
    else:
        nib = np.empty((g, 128, n, 4), np.uint8)
        nib[..., 0::2] = words & 0xF
        nib[..., 1::2] = words >> 4
        vals = E2M1[nib]
    vals = vals * np.repeat(np.exp2(scales.astype(np.float64) - 127.0), 8, axis=1)[..., None]
    return vals.transpose(0, 1, 3, 2).reshape(g * 512, n)


K, T, J, R, G, N, Z = 1024, 512, 256, 512, 32, 256, 512


def setup_inputs():
    n = np.random.standard_normal
    idx = np.stack([np.random.permutation(T)[:J] for _ in range(8)])
    idx2 = np.random.permutation(Z)[:J]
    fk = mx_kscale(K)
    fr = mx_kscale(R)
    xtp = pack_weight(n((K, T)) / fk[:, None], "e5m2")
    wp = pack_weight(n((K, R)) * 1 / np.sqrt(K) * fk[:, None] * fr, "e5m2")
    return {
        "xt_words": xtp[0],
        "xt_scales": xtp[1],
        "w_words": wp[0],
        "w_scales": wp[1],
        "wb": (n((R, N)) * 1 / np.sqrt(R) / fr[:, None]).astype(np.float32),
        "tz": (n((N, Z))).astype(np.float32),
        "offs": striped8(idx),
        "offs2": striped(idx2),
    }


def reference(xt_words, xt_scales, w_words, w_scales, wb, tz, offs, offs2):
    idx = unstriped8(offs)
    idx2 = unstriped(offs2)
    xtu = unpack_weight(xt_words, xt_scales, "e5m2")
    wu = unpack_weight(w_words, w_scales, "e5m2")
    xtidxg = pick8(xtu, idx, 64)
    a = wu.T @ xtidxg
    m1 = a.reshape(R, G, J // G).mean(axis=2)
    m2 = np.repeat(m1, J // G, axis=1)
    hid = a - m2
    wbq = mxq(f64(wb), 0, "e5m2")
    hidq = mxq(hid, 0, "e5m2")
    p = wbq.T @ hidq
    y = p * f64(tz)[:, idx2]
    return y

@@ -1,0 +1,168 @@
+from contextlib import ExitStack
+
+import concourse.mybir as mybir
+
+F32 = mybir.dt.float32
+BF16 = mybir.dt.bfloat16
+I32 = mybir.dt.int32
+U32 = mybir.dt.uint32
+U16 = mybir.dt.uint16
+U8 = mybir.dt.uint8
+E5M2X4 = mybir.dt.float8_e5m2_x4
+ALU = mybir.AluOpType
+COPY = mybir.ActivationFunctionType.Copy
+AXIS_X = mybir.AxisListType.X
+
+K, T, J, R, N, Z = 1024, 512, 256, 512, 256, 512
+FLOPS = 2 * K * R * J + 2 * R * N * J
+
+P = 128
+PASSES = 2
+SLOTS = 4
+RUN = 8
+BLOCKS = 16
+HALVES = 2
+JH = J // HALVES
+BUNDLE = 8
+LISTCOLS = JH // 16
+XS_BYTES = PASSES * J
+WS_BYTES = PASSES * R
+PLANE_BYTES = XS_BYTES + WS_BYTES
+
+
+def tile_list_headpicks_levelled_timeslook_kernel(tc, xt_words, xt_scales, w_words, w_scales, wb, tz, offs, offs2, out):
+    nc = tc.nc
+    with ExitStack() as ctx:
+        sb = ctx.enter_context(tc.tile_pool(name="sb", bufs=1))
+        ps = ctx.enter_context(tc.psum_pool(name="ps", bufs=1))
+
+        lists = sb.tile([P, J // 16], U16, name="lists")
+        list2 = sb.tile([P, J // 16], U16, name="list2")
+        xs_win = [sb.tile([P, T], U8, name="xs_win%d" % z, tag="xs_win%d" % z, align_bytes=64) for z in range(PASSES)]
+        ws_raw = sb.tile([P, WS_BYTES], U8, name="ws_raw", align_bytes=64)
+        planes = sb.tile([P, PLANE_BYTES], U8, name="planes", align_bytes=64)
+        staged = sb.tile([P, PLANE_BYTES], U8, name="staged", align_bytes=64)
+        xs_got = sb.tile([P, XS_BYTES], U8, name="xs_got", tag="xs_got", align_bytes=64)
+        xw_win = [sb.tile([P, T], I32, name="xw_win%d" % z, align_bytes=64) for z in range(PASSES)]
+        ww_raw = sb.tile([P, PASSES * R], I32, name="ww_raw", align_bytes=64)
+        ww = sb.tile([P, PASSES * R], I32, name="ww", align_bytes=64)
+        xw_got = [[sb.tile([P, JH], I32, name="xw_got%d%d" % (h, z), align_bytes=64) for z in range(PASSES)] for h in range(HALVES)]
+        wb_bf = sb.tile([P, N, SLOTS], BF16, name="wb_bf", align_bytes=64)
+        wb_words = sb.tile([P, N], U32, name="wb_words", align_bytes=64)
+        wb_plane = sb.tile([P, N], U8, name="wb_plane", align_bytes=64)
+        tz_got = sb.tile([P, 2, J], F32, name="tz_got", align_bytes=64)
+
+        for z in range(PASSES):
+            nc.vector.memset(xs_win[z][:].bitcast(I32), 0)
+        nc.gpsimd.memset(ws_raw[:].bitcast(I32), 0)
+        nc.gpsimd.memset(planes[:].bitcast(I32), 0)
+
+        nc.sync.dma_start(lists[:], offs)
+        nc.sync.dma_start(list2[:], offs2)
+        for z in range(PASSES):
+            nc.sync.dma_start(out=xs_win[z][0:P:RUN, :].bitcast(I32), in_=xt_scales[z].bitcast(I32))
+        nc.sync.dma_start(
+            out=ws_raw[0:P:RUN, :].bitcast(I32).rearrange("q (z c) -> q z c", z=PASSES),
+            in_=w_scales.bitcast(I32).rearrange("z q c -> q z c"),
+        )
+        for z in range(PASSES):
+            nc.scalar.dma_start(out=xw_win[z][:], in_=xt_words[z].rearrange("p c r -> p (c r)").bitcast(I32))
+        nc.scalar.dma_start(
+            out=ww_raw[:].rearrange("p (z c) -> p z c", z=PASSES),
+            in_=w_words.rearrange("z p c r -> p z (c r)").bitcast(I32),
+        )
+        wb_rows = wb.rearrange("(q t i) n -> t q i n", t=SLOTS, i=RUN)
+
+        for z in range(PASSES):
+            nc.vector.tensor_copy(xs_got[:, z * J : (z + 1) * J], xs_win[z][:].indirect(lists[:]))
+        wb_all = sb.tile([P, SLOTS, N], F32, name="wb_all", tag="xs_win0", align_bytes=64)
+        for t in range(SLOTS):
+            nc.scalar.dma_start(out=wb_all[:, t, :], in_=wb_rows[t])
+        nc.vector.tensor_copy(
+            out=staged[:, XS_BYTES:].bitcast(I32).rearrange("p (z t q i) -> p z t q i", z=PASSES, t=SLOTS, q=BLOCKS),
+            in_=ws_raw[:].bitcast(I32).rearrange("p (z q t i) -> p z t q i", z=PASSES, t=SLOTS, q=BLOCKS),
+        )
+        nc.vector.tensor_copy(out=staged[:, :XS_BYTES].bitcast(I32), in_=xs_got[:].bitcast(I32))
+        for x in range(4):
+            queue = nc.sync
+            queue.dma_start(
+                out=planes[32 * x : 32 * x + 4, :].bitcast(I32),
+                in_=staged[32 * x : 32 * x + 32 : RUN, :].bitcast(I32),
+            )
+        tz_win = sb.tile([P, 2, Z], F32, name="tz_win", tag="xs_got", align_bytes=64)
+        nc.sync.dma_start(out=tz_win[:], in_=tz.rearrange("(u p) z -> p u z", p=P))
+
+        def gather_words(h):
+            for z in range(PASSES):
+                nc.vector.tensor_copy(
+                    xw_got[h][z][:].bitcast(U32),
+                    xw_win[z][:].bitcast(U32).indirect(lists[:, h * LISTCOLS : (h + 1) * LISTCOLS]),
+                )
+
+        gather_words(0)
+        nc.vector.tensor_copy(
+            out=ww[:].bitcast(U32).rearrange("p (z t q i) -> p z t q i", z=PASSES, t=SLOTS, q=BLOCKS),
+            in_=ww_raw[:].bitcast(U32).rearrange("p (z q t i) -> p z t q i", z=PASSES, t=SLOTS, q=BLOCKS),
+        )
+        gather_words(1)
+
+        nc.scalar.copy(out=wb_bf[:], in_=wb_all[:].rearrange("p t n -> p n t"))
+        for u in range(2):
+            nc.scalar.activation(tz_got[:, u, :], tz_win[:, u, :].indirect(list2[:]), COPY)
+
+        a = [ps.tile([P, SLOTS, JH], F32, name="a%d" % h) for h in range(HALVES)]
+        for h in range(HALVES):
+            for t in range(SLOTS):
+                for z in range(PASSES):
+                    w0 = z * R + t * P
+                    x0 = z * J + h * JH
+                    nc.tensor.matmul_mx(
+                        out=a[h][:, t, :],
+                        lhsT=ww[:, w0 : w0 + P].bitcast(E5M2X4),
+                        lhsT_scale=planes[:, XS_BYTES + w0 : XS_BYTES + w0 + P],
+                        rhs=xw_got[h][z][:].bitcast(E5M2X4),
+                        rhs_scale=planes[:, x0 : x0 + JH],
+                        start=(z == 0),
+                        stop=(z == PASSES - 1),
+                    )
+
+        nc.vector.quantize_mx(
+            out=wb_words[:].bitcast(E5M2X4), scales=wb_plane[:], in_=wb_bf[:].rearrange("p n t -> p (n t)")
+        )
+
+        GH = JH // BUNDLE
+        for h in range(HALVES):
+            sums = sb.tile([P, GH, SLOTS], F32, name="sums%d" % h)
+            means = sb.tile([P, GH, SLOTS], F32, name="means%d" % h)
+            hid = sb.tile([P, GH, BUNDLE, SLOTS], BF16, name="hid%d" % h, align_bytes=64)
+            hid_words = sb.tile([P, JH], U32, name="hid_words%d" % h, align_bytes=64)
+            hid_plane = sb.tile([P, JH], U8, name="hid_plane%d" % h, align_bytes=64)
+            y = sb.tile([P, 2, JH], F32, name="y%d" % h, align_bytes=64)
+            p = ps.tile([P, 2, JH], F32, name="p%d" % h)
+            nc.vector.tensor_reduce(
+                out=sums[:], in_=a[h][:].rearrange("p t (g i) -> p g t i", i=BUNDLE), axis=AXIS_X, op=ALU.add
+            )
+            nc.vector.tensor_scalar(out=means[:], in0=sums[:], scalar1=1.0 / BUNDLE, scalar2=None, op0=ALU.mult)
+            nc.vector.tensor_tensor(
+                out=hid[:],
+                in0=a[h][:].rearrange("p t (g i) -> p g i t", i=BUNDLE),
+                in1=means[:].unsqueeze(2).to_broadcast([P, GH, BUNDLE, SLOTS]),
+                op=ALU.subtract,
+            )
+            nc.vector.quantize_mx(
+                out=hid_words[:].bitcast(E5M2X4), scales=hid_plane[:], in_=hid[:].rearrange("p g i t -> p (g i t)")
+            )
+            for u in range(2):
+                nc.tensor.matmul_mx(
+                    out=p[:, u, :],
+                    lhsT=wb_words[:, u * P : (u + 1) * P].bitcast(E5M2X4),
+                    lhsT_scale=wb_plane[:, u * P : (u + 1) * P],
+                    rhs=hid_words[:].bitcast(E5M2X4),
+                    rhs_scale=hid_plane[:],
+                    start=True,
+                    stop=True,
+                )
+            nc.vector.tensor_tensor(out=y[:], in0=p[:], in1=tz_got[:, :, h * JH : (h + 1) * JH], op=ALU.mult)
+            nc.sync.dma_start(
+                out=out[:, h * JH : (h + 1) * JH].rearrange("(u p) j -> p u j", p=P), in_=y[:]
+            )

@@ -43,41 +43,51 @@ def tile_list_headpicks_levelled_timeslook_kernel(tc, xt_words, xt_scales, w_wor
         planes = sb.tile([P, PLANE_BYTES], U8, name="planes", align_bytes=64)
         staged = sb.tile([P, PLANE_BYTES], U8, name="staged", align_bytes=64)
         xs_got = sb.tile([P, XS_BYTES], U8, name="xs_got", tag="xs_got", align_bytes=64)
-        xw_win = [sb.tile([P, T], I32, name="xw_win%d" % z, align_bytes=64) for z in range(PASSES)]
-        ww_raw = sb.tile([P, PASSES * R], I32, name="ww_raw", align_bytes=64)
+        xw_win = [sb.tile([P, T], I32, name="xw_win%d" % z, tag="xw_win%d" % z, align_bytes=64) for z in range(PASSES)]
+        ww_raw = sb.tile([P, PASSES * R], I32, name="ww_raw", tag="ww_raw", align_bytes=64)
         ww = sb.tile([P, PASSES * R], I32, name="ww", align_bytes=64)
         xw_got = [[sb.tile([P, JH], I32, name="xw_got%d%d" % (h, z), align_bytes=64) for z in range(PASSES)] for h in range(HALVES)]
         wb_bf = sb.tile([P, N, SLOTS], BF16, name="wb_bf", align_bytes=64)
         wb_words = sb.tile([P, N], U32, name="wb_words", align_bytes=64)
         wb_plane = sb.tile([P, N], U8, name="wb_plane", align_bytes=64)
-        tz_got = sb.tile([P, 2, J], F32, name="tz_got", align_bytes=64)
+        tz_got = [sb.tile([P, 2, JH], F32, name="tz_got%d" % h, align_bytes=64) for h in range(HALVES)]
 
-        for z in range(PASSES):
-            nc.vector.memset(xs_win[z][:].bitcast(I32), 0)
-        nc.gpsimd.memset(ws_raw[:].bitcast(I32), 0)
-        nc.gpsimd.memset(planes[:].bitcast(I32), 0)
+        nc.vector.memset(ws_raw[:, :R].bitcast(I32), 0)
+        nc.gpsimd.memset(ws_raw[:, R:].bitcast(I32), 0)
+        nc.vector.memset(planes[:].bitcast(I32), 0)
+        warm_in = sb.tile([P, 1], F32, name="warm_in")
+        warm_out = sb.tile([P, 1], F32, name="warm_out")
+        nc.gpsimd.memset(warm_in[:], 0.0)
 
         nc.sync.dma_start(lists[:], offs)
-        nc.sync.dma_start(list2[:], offs2)
         for z in range(PASSES):
-            nc.sync.dma_start(out=xs_win[z][0:P:RUN, :].bitcast(I32), in_=xt_scales[z].bitcast(I32))
+            nc.scalar.dma_start(
+                out=xs_win[z][:].bitcast(I32),
+                in_=xt_scales[z].bitcast(I32).unsqueeze(1).to_broadcast([BLOCKS, RUN, T // 4]),
+            )
+        nc.sync.dma_start(list2[:], offs2)
         nc.sync.dma_start(
             out=ws_raw[0:P:RUN, :].bitcast(I32).rearrange("q (z c) -> q z c", z=PASSES),
             in_=w_scales.bitcast(I32).rearrange("z q c -> q z c"),
         )
         for z in range(PASSES):
-            nc.scalar.dma_start(out=xw_win[z][:], in_=xt_words[z].rearrange("p c r -> p (c r)").bitcast(I32))
-        nc.scalar.dma_start(
+            nc.sync.dma_start(out=xw_win[z][:], in_=xt_words[z].rearrange("p c r -> p (c r)").bitcast(I32))
+        nc.sync.dma_start(
             out=ww_raw[:].rearrange("p (z c) -> p z c", z=PASSES),
             in_=w_words.rearrange("z p c r -> p z (c r)").bitcast(I32),
         )
+        nc.scalar.activation(warm_out[:], warm_in[:], COPY)
         wb_rows = wb.rearrange("(q t i) n -> t q i n", t=SLOTS, i=RUN)
 
         for z in range(PASSES):
             nc.vector.tensor_copy(xs_got[:, z * J : (z + 1) * J], xs_win[z][:].indirect(lists[:]))
-        wb_all = sb.tile([P, SLOTS, N], F32, name="wb_all", tag="xs_win0", align_bytes=64)
-        for t in range(SLOTS):
-            nc.scalar.dma_start(out=wb_all[:, t, :], in_=wb_rows[t])
+        def load_wb_pair(pair, tag):
+            rows = sb.tile([P, 2, N], F32, name="wb_pair%d" % pair, tag=tag, align_bytes=64)
+            for e in range(2):
+                nc.scalar.dma_start(out=rows[:, e, :], in_=wb_rows[2 * pair + e])
+            return rows
+
+        wb_pairs = [load_wb_pair(0, "xs_win0")]
         nc.vector.tensor_copy(
             out=staged[:, XS_BYTES:].bitcast(I32).rearrange("p (z t q i) -> p z t q i", z=PASSES, t=SLOTS, q=BLOCKS),
             in_=ws_raw[:].bitcast(I32).rearrange("p (z q t i) -> p z t q i", z=PASSES, t=SLOTS, q=BLOCKS),
@@ -89,8 +99,6 @@ def tile_list_headpicks_levelled_timeslook_kernel(tc, xt_words, xt_scales, w_wor
                 out=planes[32 * x : 32 * x + 4, :].bitcast(I32),
                 in_=staged[32 * x : 32 * x + 32 : RUN, :].bitcast(I32),
             )
-        tz_win = sb.tile([P, 2, Z], F32, name="tz_win", tag="xs_got", align_bytes=64)
-        nc.sync.dma_start(out=tz_win[:], in_=tz.rearrange("(u p) z -> p u z", p=P))
 
         def gather_words(h):
             for z in range(PASSES):
@@ -104,11 +112,18 @@ def tile_list_headpicks_levelled_timeslook_kernel(tc, xt_words, xt_scales, w_wor
             out=ww[:].bitcast(U32).rearrange("p (z t q i) -> p z t q i", z=PASSES, t=SLOTS, q=BLOCKS),
             in_=ww_raw[:].bitcast(U32).rearrange("p (z q t i) -> p z t q i", z=PASSES, t=SLOTS, q=BLOCKS),
         )
+        wb_pairs.append(load_wb_pair(1, "ww_raw"))
         gather_words(1)
+        tz_win = sb.tile([P, 2, Z], F32, name="tz_win", tag="xw_win0", align_bytes=64)
+        nc.sync.dma_start(out=tz_win[:], in_=tz.rearrange("(u p) z -> p u z", p=P))
 
-        nc.scalar.copy(out=wb_bf[:], in_=wb_all[:].rearrange("p t n -> p n t"))
-        for u in range(2):
-            nc.scalar.activation(tz_got[:, u, :], tz_win[:, u, :].indirect(list2[:]), COPY)
+        for pair in range(2):
+            nc.scalar.copy(out=wb_bf[:, :, 2 * pair : 2 * pair + 2], in_=wb_pairs[pair][:].rearrange("p e n -> p n e"))
+        for h in range(HALVES):
+            for u in range(2):
+                nc.scalar.activation(
+                    tz_got[h][:, u, :], tz_win[:, u, :].indirect(list2[:, h * LISTCOLS : (h + 1) * LISTCOLS]), COPY
+                )
 
         a = [ps.tile([P, SLOTS, JH], F32, name="a%d" % h) for h in range(HALVES)]
         for h in range(HALVES):
@@ -137,12 +152,10 @@ def tile_list_headpicks_levelled_timeslook_kernel(tc, xt_words, xt_scales, w_wor
             hid = sb.tile([P, GH, BUNDLE, SLOTS], BF16, name="hid%d" % h, align_bytes=64)
             hid_words = sb.tile([P, JH], U32, name="hid_words%d" % h, align_bytes=64)
             hid_plane = sb.tile([P, JH], U8, name="hid_plane%d" % h, align_bytes=64)
-            y = sb.tile([P, 2, JH], F32, name="y%d" % h, align_bytes=64)
-            p = ps.tile([P, 2, JH], F32, name="p%d" % h)
             nc.vector.tensor_reduce(
                 out=sums[:], in_=a[h][:].rearrange("p t (g i) -> p g t i", i=BUNDLE), axis=AXIS_X, op=ALU.add
             )
-            nc.vector.tensor_scalar(out=means[:], in0=sums[:], scalar1=1.0 / BUNDLE, scalar2=None, op0=ALU.mult)
+            nc.gpsimd.tensor_scalar(out=means[:], in0=sums[:], scalar1=1.0 / BUNDLE, scalar2=0.0, op0=ALU.mult, op1=ALU.add)
             nc.vector.tensor_tensor(
                 out=hid[:],
                 in0=a[h][:].rearrange("p t (g i) -> p g i t", i=BUNDLE),
@@ -152,17 +165,23 @@ def tile_list_headpicks_levelled_timeslook_kernel(tc, xt_words, xt_scales, w_wor
             nc.vector.quantize_mx(
                 out=hid_words[:].bitcast(E5M2X4), scales=hid_plane[:], in_=hid[:].rearrange("p g i t -> p (g i t)")
             )
-            for u in range(2):
-                nc.tensor.matmul_mx(
-                    out=p[:, u, :],
-                    lhsT=wb_words[:, u * P : (u + 1) * P].bitcast(E5M2X4),
-                    lhsT_scale=wb_plane[:, u * P : (u + 1) * P],
-                    rhs=hid_words[:].bitcast(E5M2X4),
-                    rhs_scale=hid_plane[:],
-                    start=True,
-                    stop=True,
+            pieces = [range(2)] if h < HALVES - 1 else [range(0, 1), range(1, 2)]
+            for us in pieces:
+                p = ps.tile([P, len(us), JH], F32, name="p%d%d" % (h, us.start))
+                y = sb.tile([P, len(us), JH], F32, name="y%d%d" % (h, us.start), align_bytes=64)
+                for u in us:
+                    nc.tensor.matmul_mx(
+                        out=p[:, u - us.start, :],
+                        lhsT=wb_words[:, u * P : (u + 1) * P].bitcast(E5M2X4),
+                        lhsT_scale=wb_plane[:, u * P : (u + 1) * P],
+                        rhs=hid_words[:].bitcast(E5M2X4),
+                        rhs_scale=hid_plane[:],
+                        start=True,
+                        stop=True,
+                    )
+                nc.vector.tensor_tensor(out=y[:], in0=p[:], in1=tz_got[h][:, us.start : us.stop, :], op=ALU.mult)
+                queue = nc.scalar if us.start else nc.sync
+                queue.dma_start(
+                    out=out[us.start * P : us.stop * P, h * JH : (h + 1) * JH].rearrange("(u p) j -> p u j", p=P),
+                    in_=y[:],
                 )
-            nc.vector.tensor_tensor(out=y[:], in0=p[:], in1=tz_got[:, :, h * JH : (h + 1) * JH], op=ALU.mult)
-            nc.sync.dma_start(
-                out=out[:, h * JH : (h + 1) * JH].rearrange("(u p) j -> p u j", p=P), in_=y[:]
-            )

@@ -41,27 +41,25 @@ def tile_list_headpicks_levelled_timeslook_kernel(tc, xt_words, xt_scales, w_wor
         xs_win = [sb.tile([P, T], U8, name="xs_win%d" % z, tag="xs_win%d" % z, align_bytes=64) for z in range(PASSES)]
         ws_raw = sb.tile([P, WS_BYTES], U8, name="ws_raw", align_bytes=64)
         planes = sb.tile([P, PLANE_BYTES], U8, name="planes", align_bytes=64)
-        staged = sb.tile([P, PLANE_BYTES], U8, name="staged", align_bytes=64)
         xs_got = sb.tile([P, XS_BYTES], U8, name="xs_got", tag="xs_got", align_bytes=64)
         xw_win = [sb.tile([P, T], I32, name="xw_win%d" % z, tag="xw_win%d" % z, align_bytes=64) for z in range(PASSES)]
         ww_raw = sb.tile([P, PASSES * R], I32, name="ww_raw", tag="ww_raw", align_bytes=64)
         ww = sb.tile([P, PASSES * R], I32, name="ww", align_bytes=64)
-        xw_got = [[sb.tile([P, JH], I32, name="xw_got%d%d" % (h, z), align_bytes=64) for z in range(PASSES)] for h in range(HALVES)]
+        xw_got = [[sb.tile([P, JH], I32, name="xw_got%d%d" % (h, z), tag="xw_got%d%d" % (h, z), align_bytes=64) for z in range(PASSES)] for h in range(HALVES)]
         wb_bf = sb.tile([P, N, SLOTS], BF16, name="wb_bf", align_bytes=64)
-        wb_words = sb.tile([P, N], U32, name="wb_words", align_bytes=64)
         wb_plane = sb.tile([P, N], U8, name="wb_plane", align_bytes=64)
         tz_got = [sb.tile([P, 2, JH], F32, name="tz_got%d" % h, align_bytes=64) for h in range(HALVES)]
 
         nc.vector.memset(ws_raw[:, :R].bitcast(I32), 0)
         nc.gpsimd.memset(ws_raw[:, R:].bitcast(I32), 0)
-        nc.vector.memset(planes[:].bitcast(I32), 0)
         warm_in = sb.tile([P, 1], F32, name="warm_in")
         warm_out = sb.tile([P, 1], F32, name="warm_out")
         nc.gpsimd.memset(warm_in[:], 0.0)
 
         nc.sync.dma_start(lists[:], offs)
         for z in range(PASSES):
-            nc.scalar.dma_start(
+            queue = nc.sync if z else nc.scalar
+            queue.dma_start(
                 out=xs_win[z][:].bitcast(I32),
                 in_=xt_scales[z].bitcast(I32).unsqueeze(1).to_broadcast([BLOCKS, RUN, T // 4]),
             )
@@ -81,24 +79,17 @@ def tile_list_headpicks_levelled_timeslook_kernel(tc, xt_words, xt_scales, w_wor
 
         for z in range(PASSES):
             nc.vector.tensor_copy(xs_got[:, z * J : (z + 1) * J], xs_win[z][:].indirect(lists[:]))
-        def load_wb_pair(pair, tag):
-            rows = sb.tile([P, 2, N], F32, name="wb_pair%d" % pair, tag=tag, align_bytes=64)
-            for e in range(2):
-                nc.scalar.dma_start(out=rows[:, e, :], in_=wb_rows[2 * pair + e])
-            return rows
-
-        wb_pairs = [load_wb_pair(0, "xs_win0")]
+        wb_raw = sb.tile([P, SLOTS, N], F32, name="wb_raw", tag="xs_win0", align_bytes=64)
+        for t in range(SLOTS):
+            nc.scalar.dma_start(out=wb_raw[:, t, :], in_=wb_rows[t])
         nc.vector.tensor_copy(
-            out=staged[:, XS_BYTES:].bitcast(I32).rearrange("p (z t q i) -> p z t q i", z=PASSES, t=SLOTS, q=BLOCKS),
+            out=planes[:, XS_BYTES:].bitcast(I32).rearrange("p (z t q i) -> p z t q i", z=PASSES, t=SLOTS, q=BLOCKS),
             in_=ws_raw[:].bitcast(I32).rearrange("p (z q t i) -> p z t q i", z=PASSES, t=SLOTS, q=BLOCKS),
         )
-        nc.vector.tensor_copy(out=staged[:, :XS_BYTES].bitcast(I32), in_=xs_got[:].bitcast(I32))
-        for x in range(4):
-            queue = nc.sync
-            queue.dma_start(
-                out=planes[32 * x : 32 * x + 4, :].bitcast(I32),
-                in_=staged[32 * x : 32 * x + 32 : RUN, :].bitcast(I32),
-            )
+        nc.vector.tensor_copy(out=planes[:, :XS_BYTES].bitcast(I32), in_=xs_got[:].bitcast(I32))
+        for r in range(1, 4):
+            queue = nc.sync if r % 2 else nc.scalar
+            queue.dma_start(out=planes[r:P:32, :].bitcast(I32), in_=planes[RUN * r : P : 32, :].bitcast(I32))
 
         def gather_words(h):
             for z in range(PASSES):
@@ -112,13 +103,11 @@ def tile_list_headpicks_levelled_timeslook_kernel(tc, xt_words, xt_scales, w_wor
             out=ww[:].bitcast(U32).rearrange("p (z t q i) -> p z t q i", z=PASSES, t=SLOTS, q=BLOCKS),
             in_=ww_raw[:].bitcast(U32).rearrange("p (z q t i) -> p z t q i", z=PASSES, t=SLOTS, q=BLOCKS),
         )
-        wb_pairs.append(load_wb_pair(1, "ww_raw"))
-        gather_words(1)
-        tz_win = sb.tile([P, 2, Z], F32, name="tz_win", tag="xw_win0", align_bytes=64)
+        tz_win = sb.tile([P, 2, Z], F32, name="tz_win", tag="ww_raw", align_bytes=64)
         nc.sync.dma_start(out=tz_win[:], in_=tz.rearrange("(u p) z -> p u z", p=P))
+        gather_words(1)
 
-        for pair in range(2):
-            nc.scalar.copy(out=wb_bf[:, :, 2 * pair : 2 * pair + 2], in_=wb_pairs[pair][:].rearrange("p e n -> p n e"))
+        nc.scalar.copy(out=wb_bf[:], in_=wb_raw[:].rearrange("p t n -> p n t"))
         for h in range(HALVES):
             for u in range(2):
                 nc.scalar.activation(
@@ -141,9 +130,6 @@ def tile_list_headpicks_levelled_timeslook_kernel(tc, xt_words, xt_scales, w_wor
                         stop=(z == PASSES - 1),
                     )
 
-        nc.vector.quantize_mx(
-            out=wb_words[:].bitcast(E5M2X4), scales=wb_plane[:], in_=wb_bf[:].rearrange("p n t -> p (n t)")
-        )
 
         GH = JH // BUNDLE
         for h in range(HALVES):
@@ -155,6 +141,11 @@ def tile_list_headpicks_levelled_timeslook_kernel(tc, xt_words, xt_scales, w_wor
             nc.vector.tensor_reduce(
                 out=sums[:], in_=a[h][:].rearrange("p t (g i) -> p g t i", i=BUNDLE), axis=AXIS_X, op=ALU.add
             )
+            if h == 0:
+                wb_words = sb.tile([P, N], U32, name="wb_words", tag="xw_got01", align_bytes=64)
+                nc.vector.quantize_mx(
+                    out=wb_words[:].bitcast(E5M2X4), scales=wb_plane[:], in_=wb_bf[:].rearrange("p n t -> p (n t)")
+                )
             nc.gpsimd.tensor_scalar(out=means[:], in0=sums[:], scalar1=1.0 / BUNDLE, scalar2=0.0, op0=ALU.mult, op1=ALU.add)
             nc.vector.tensor_tensor(
                 out=hid[:],

@@ -48,7 +48,6 @@ def tile_list_headpicks_levelled_timeslook_kernel(tc, xt_words, xt_scales, w_wor
         xw_got = [[sb.tile([P, JH], I32, name="xw_got%d%d" % (h, z), tag="xw_got%d%d" % (h, z), align_bytes=64) for z in range(PASSES)] for h in range(HALVES)]
         wb_bf = sb.tile([P, N, SLOTS], BF16, name="wb_bf", align_bytes=64)
         wb_plane = sb.tile([P, N], U8, name="wb_plane", align_bytes=64)
-        tz_got = [sb.tile([P, 2, JH], F32, name="tz_got%d" % h, align_bytes=64) for h in range(HALVES)]
 
         nc.vector.memset(ws_raw[:, :R].bitcast(I32), 0)
         nc.gpsimd.memset(ws_raw[:, R:].bitcast(I32), 0)
@@ -108,11 +107,6 @@ def tile_list_headpicks_levelled_timeslook_kernel(tc, xt_words, xt_scales, w_wor
         gather_words(1)
 
         nc.scalar.copy(out=wb_bf[:], in_=wb_raw[:].rearrange("p t n -> p n t"))
-        for h in range(HALVES):
-            for u in range(2):
-                nc.scalar.activation(
-                    tz_got[h][:, u, :], tz_win[:, u, :].indirect(list2[:, h * LISTCOLS : (h + 1) * LISTCOLS]), COPY
-                )
 
         a = [ps.tile([P, SLOTS, JH], F32, name="a%d" % h) for h in range(HALVES)]
         for h in range(HALVES):
@@ -132,12 +126,9 @@ def tile_list_headpicks_levelled_timeslook_kernel(tc, xt_words, xt_scales, w_wor
 
 
         GH = JH // BUNDLE
+        means = [sb.tile([P, GH, SLOTS], F32, name="means%d" % h) for h in range(HALVES)]
         for h in range(HALVES):
-            sums = sb.tile([P, GH, SLOTS], F32, name="sums%d" % h)
-            means = sb.tile([P, GH, SLOTS], F32, name="means%d" % h)
-            hid = sb.tile([P, GH, BUNDLE, SLOTS], BF16, name="hid%d" % h, align_bytes=64)
-            hid_words = sb.tile([P, JH], U32, name="hid_words%d" % h, align_bytes=64)
-            hid_plane = sb.tile([P, JH], U8, name="hid_plane%d" % h, align_bytes=64)
+            sums = sb.tile([P, GH, SLOTS], F32, name="sums%d" % h, tag="sums%d" % h, align_bytes=64)
             nc.vector.tensor_reduce(
                 out=sums[:], in_=a[h][:].rearrange("p t (g i) -> p g t i", i=BUNDLE), axis=AXIS_X, op=ALU.add
             )
@@ -146,15 +137,29 @@ def tile_list_headpicks_levelled_timeslook_kernel(tc, xt_words, xt_scales, w_wor
                 nc.vector.quantize_mx(
                     out=wb_words[:].bitcast(E5M2X4), scales=wb_plane[:], in_=wb_bf[:].rearrange("p n t -> p (n t)")
                 )
-            nc.gpsimd.tensor_scalar(out=means[:], in0=sums[:], scalar1=1.0 / BUNDLE, scalar2=0.0, op0=ALU.mult, op1=ALU.add)
+            nc.scalar.activation(means[h][:], sums[:], COPY, scale=1.0 / BUNDLE)
+
+        tz_got = sb.tile([P, HALVES, 2, JH], F32, name="tz_got", tag="sums1", align_bytes=64)
+        for h in range(HALVES):
+            for u in range(2):
+                nc.scalar.activation(
+                    tz_got[:, h, u, :], tz_win[:, u, :].indirect(list2[:, h * LISTCOLS : (h + 1) * LISTCOLS]), COPY
+                )
+
+        hid = [sb.tile([P, GH, BUNDLE, SLOTS], BF16, name="hid%d" % h, align_bytes=64) for h in range(HALVES)]
+        for h in range(HALVES):
             nc.vector.tensor_tensor(
-                out=hid[:],
+                out=hid[h][:],
                 in0=a[h][:].rearrange("p t (g i) -> p g i t", i=BUNDLE),
-                in1=means[:].unsqueeze(2).to_broadcast([P, GH, BUNDLE, SLOTS]),
+                in1=means[h][:].unsqueeze(2).to_broadcast([P, GH, BUNDLE, SLOTS]),
                 op=ALU.subtract,
             )
+
+        for h in range(HALVES):
+            hid_words = sb.tile([P, JH], U32, name="hid_words%d" % h, align_bytes=64)
+            hid_plane = sb.tile([P, JH], U8, name="hid_plane%d" % h, align_bytes=64)
             nc.vector.quantize_mx(
-                out=hid_words[:].bitcast(E5M2X4), scales=hid_plane[:], in_=hid[:].rearrange("p g i t -> p (g i t)")
+                out=hid_words[:].bitcast(E5M2X4), scales=hid_plane[:], in_=hid[h][:].rearrange("p g i t -> p (g i t)")
             )
             pieces = [range(2)] if h < HALVES - 1 else [range(0, 1), range(1, 2)]
             for us in pieces:
@@ -170,7 +175,7 @@ def tile_list_headpicks_levelled_timeslook_kernel(tc, xt_words, xt_scales, w_wor
                         start=True,
                         stop=True,
                     )
-                nc.vector.tensor_tensor(out=y[:], in0=p[:], in1=tz_got[h][:, us.start : us.stop, :], op=ALU.mult)
+                nc.vector.tensor_tensor(out=y[:], in0=p[:], in1=tz_got[:, h, us.start : us.stop, :], op=ALU.mult)
                 queue = nc.scalar if us.start else nc.sync
                 queue.dma_start(
                     out=out[us.start * P : us.stop * P, h * JH : (h + 1) * JH].rearrange("(u p) j -> p u j", p=P),

from contextlib import ExitStack

import concourse.mybir as mybir

F32 = mybir.dt.float32
BF16 = mybir.dt.bfloat16
I32 = mybir.dt.int32
U32 = mybir.dt.uint32
U16 = mybir.dt.uint16
U8 = mybir.dt.uint8
E5M2X4 = mybir.dt.float8_e5m2_x4
ALU = mybir.AluOpType
COPY = mybir.ActivationFunctionType.Copy
AXIS_X = mybir.AxisListType.X

K, T, J, R, N, Z = 1024, 512, 256, 512, 256, 512
FLOPS = 2 * K * R * J + 2 * R * N * J

P = 128
PASSES = 2
SLOTS = 4
RUN = 8
BLOCKS = 16
HALVES = 2
JH = J // HALVES
BUNDLE = 8
LISTCOLS = JH // 16
XS_BYTES = PASSES * J
WS_BYTES = PASSES * R
PLANE_BYTES = XS_BYTES + WS_BYTES


def tile_list_headpicks_levelled_timeslook_kernel(tc, xt_words, xt_scales, w_words, w_scales, wb, tz, offs, offs2, out):
    nc = tc.nc
    with ExitStack() as ctx:
        sb = ctx.enter_context(tc.tile_pool(name="sb", bufs=1))
        ps = ctx.enter_context(tc.psum_pool(name="ps", bufs=1))

        lists = sb.tile([P, J // 16], U16, name="lists")
        list2 = sb.tile([P, J // 16], U16, name="list2")
        xs_win = [sb.tile([P, T], U8, name="xs_win%d" % z, tag="xs_win%d" % z, align_bytes=64) for z in range(PASSES)]
        ws_raw = sb.tile([P, WS_BYTES], U8, name="ws_raw", align_bytes=64)
        planes = sb.tile([P, PLANE_BYTES], U8, name="planes", align_bytes=64)
        xs_got = sb.tile([P, XS_BYTES], U8, name="xs_got", tag="xs_got", align_bytes=64)
        xw_win = [sb.tile([P, T], I32, name="xw_win%d" % z, tag="xw_win%d" % z, align_bytes=64) for z in range(PASSES)]
        ww_raw = sb.tile([P, PASSES * R], I32, name="ww_raw", tag="ww_raw", align_bytes=64)
        ww = sb.tile([P, PASSES * R], I32, name="ww", align_bytes=64)
        xw_got = [[sb.tile([P, JH], I32, name="xw_got%d%d" % (h, z), tag="xw_got%d%d" % (h, z), align_bytes=64) for z in range(PASSES)] for h in range(HALVES)]
        wb_bf = sb.tile([P, N, SLOTS], BF16, name="wb_bf", align_bytes=64)
        wb_plane = sb.tile([P, N], U8, name="wb_plane", align_bytes=64)

        nc.vector.memset(ws_raw[:, :R].bitcast(I32), 0)
        nc.gpsimd.memset(ws_raw[:, R:].bitcast(I32), 0)
        warm_in = sb.tile([P, 1], F32, name="warm_in")
        warm_out = sb.tile([P, 1], F32, name="warm_out")
        nc.gpsimd.memset(warm_in[:], 0.0)

        nc.sync.dma_start(lists[:], offs)
        for z in range(PASSES):
            queue = nc.sync if z else nc.scalar
            queue.dma_start(
                out=xs_win[z][:].bitcast(I32),
                in_=xt_scales[z].bitcast(I32).unsqueeze(1).to_broadcast([BLOCKS, RUN, T // 4]),
            )
        nc.sync.dma_start(list2[:], offs2)
        nc.sync.dma_start(
            out=ws_raw[0:P:RUN, :].bitcast(I32).rearrange("q (z c) -> q z c", z=PASSES),
            in_=w_scales.bitcast(I32).rearrange("z q c -> q z c"),
        )
        for z in range(PASSES):
            nc.sync.dma_start(out=xw_win[z][:], in_=xt_words[z].rearrange("p c r -> p (c r)").bitcast(I32))
        nc.sync.dma_start(
            out=ww_raw[:].rearrange("p (z c) -> p z c", z=PASSES),
            in_=w_words.rearrange("z p c r -> p z (c r)").bitcast(I32),
        )
        nc.scalar.activation(warm_out[:], warm_in[:], COPY)
        wb_rows = wb.rearrange("(q t i) n -> t q i n", t=SLOTS, i=RUN)

        for z in range(PASSES):
            nc.vector.tensor_copy(xs_got[:, z * J : (z + 1) * J], xs_win[z][:].indirect(lists[:]))
        wb_raw = sb.tile([P, SLOTS, N], F32, name="wb_raw", tag="xs_win0", align_bytes=64)
        for t in range(SLOTS):
            nc.scalar.dma_start(out=wb_raw[:, t, :], in_=wb_rows[t])
        nc.vector.tensor_copy(
            out=planes[:, XS_BYTES:].bitcast(I32).rearrange("p (z t q i) -> p z t q i", z=PASSES, t=SLOTS, q=BLOCKS),
            in_=ws_raw[:].bitcast(I32).rearrange("p (z q t i) -> p z t q i", z=PASSES, t=SLOTS, q=BLOCKS),
        )
        nc.vector.tensor_copy(out=planes[:, :XS_BYTES].bitcast(I32), in_=xs_got[:].bitcast(I32))
        for r in range(1, 4):
            queue = nc.sync if r % 2 else nc.scalar
            queue.dma_start(out=planes[r:P:32, :].bitcast(I32), in_=planes[RUN * r : P : 32, :].bitcast(I32))

        def gather_words(h):
            for z in range(PASSES):
                nc.vector.tensor_copy(
                    xw_got[h][z][:].bitcast(U32),
                    xw_win[z][:].bitcast(U32).indirect(lists[:, h * LISTCOLS : (h + 1) * LISTCOLS]),
                )

        gather_words(0)
        nc.vector.tensor_copy(
            out=ww[:].bitcast(U32).rearrange("p (z t q i) -> p z t q i", z=PASSES, t=SLOTS, q=BLOCKS),
            in_=ww_raw[:].bitcast(U32).rearrange("p (z q t i) -> p z t q i", z=PASSES, t=SLOTS, q=BLOCKS),
        )
        tz_win = sb.tile([P, 2, Z], F32, name="tz_win", tag="ww_raw", align_bytes=64)
        nc.sync.dma_start(out=tz_win[:], in_=tz.rearrange("(u p) z -> p u z", p=P))
        gather_words(1)

        nc.scalar.copy(out=wb_bf[:], in_=wb_raw[:].rearrange("p t n -> p n t"))

        a = [ps.tile([P, SLOTS, JH], F32, name="a%d" % h) for h in range(HALVES)]
        for h in range(HALVES):
            for t in range(SLOTS):
                for z in range(PASSES):
                    w0 = z * R + t * P
                    x0 = z * J + h * JH
                    nc.tensor.matmul_mx(
                        out=a[h][:, t, :],
                        lhsT=ww[:, w0 : w0 + P].bitcast(E5M2X4),
                        lhsT_scale=planes[:, XS_BYTES + w0 : XS_BYTES + w0 + P],
                        rhs=xw_got[h][z][:].bitcast(E5M2X4),
                        rhs_scale=planes[:, x0 : x0 + JH],
                        start=(z == 0),
                        stop=(z == PASSES - 1),
                    )


        GH = JH // BUNDLE
        means = [sb.tile([P, GH, SLOTS], F32, name="means%d" % h) for h in range(HALVES)]
        for h in range(HALVES):
            sums = sb.tile([P, GH, SLOTS], F32, name="sums%d" % h, tag="sums%d" % h, align_bytes=64)
            nc.vector.tensor_reduce(
                out=sums[:], in_=a[h][:].rearrange("p t (g i) -> p g t i", i=BUNDLE), axis=AXIS_X, op=ALU.add
            )
            if h == 0:
                wb_words = sb.tile([P, N], U32, name="wb_words", tag="xw_got01", align_bytes=64)
                nc.vector.quantize_mx(
                    out=wb_words[:].bitcast(E5M2X4), scales=wb_plane[:], in_=wb_bf[:].rearrange("p n t -> p (n t)")
                )
            nc.scalar.activation(means[h][:], sums[:], COPY, scale=1.0 / BUNDLE)

        tz_got = sb.tile([P, HALVES, 2, JH], F32, name="tz_got", tag="sums1", align_bytes=64)
        for h in range(HALVES):
            for u in range(2):
                nc.scalar.activation(
                    tz_got[:, h, u, :], tz_win[:, u, :].indirect(list2[:, h * LISTCOLS : (h + 1) * LISTCOLS]), COPY
                )

        hid = [sb.tile([P, GH, BUNDLE, SLOTS], BF16, name="hid%d" % h, align_bytes=64) for h in range(HALVES)]
        for h in range(HALVES):
            nc.vector.tensor_tensor(
                out=hid[h][:],
                in0=a[h][:].rearrange("p t (g i) -> p g i t", i=BUNDLE),
                in1=means[h][:].unsqueeze(2).to_broadcast([P, GH, BUNDLE, SLOTS]),
                op=ALU.subtract,
            )

        for h in range(HALVES):
            hid_words = sb.tile([P, JH], U32, name="hid_words%d" % h, align_bytes=64)
            hid_plane = sb.tile([P, JH], U8, name="hid_plane%d" % h, align_bytes=64)
            nc.vector.quantize_mx(
                out=hid_words[:].bitcast(E5M2X4), scales=hid_plane[:], in_=hid[h][:].rearrange("p g i t -> p (g i t)")
            )
            pieces = [range(2)] if h < HALVES - 1 else [range(0, 1), range(1, 2)]
            for us in pieces:
                p = ps.tile([P, len(us), JH], F32, name="p%d%d" % (h, us.start))
                y = sb.tile([P, len(us), JH], F32, name="y%d%d" % (h, us.start), align_bytes=64)
                for u in us:
                    nc.tensor.matmul_mx(
                        out=p[:, u - us.start, :],
                        lhsT=wb_words[:, u * P : (u + 1) * P].bitcast(E5M2X4),
                        lhsT_scale=wb_plane[:, u * P : (u + 1) * P],
                        rhs=hid_words[:].bitcast(E5M2X4),
                        rhs_scale=hid_plane[:],
                        start=True,
                        stop=True,
                    )
                nc.vector.tensor_tensor(out=y[:], in0=p[:], in1=tz_got[:, h, us.start : us.stop, :], op=ALU.mult)
                queue = nc.scalar if us.start else nc.sync
                queue.dma_start(
                    out=out[us.start * P : us.stop * P, h * JH : (h + 1) * JH].rearrange("(u p) j -> p u j", p=P),
                    in_=y[:],
                )
